import numpy as np, ml_dtypes
CORES = [125,127,253,255,381,383,509,511]
N = 8
R, T = 8192, 1024
HOST = [c // 128 for c in CORES]
G = [[r for r in range(N) if HOST[r] == h] for h in sorted(set(HOST))]
H = len(G); K = [sorted(set(HOST)).index(h) for h in HOST]
def entries(a): return a.T.reshape(-1)
def pack(v, P): return np.ascontiguousarray(np.asarray(v, np.int32).reshape(-1, P).T)
def among(rng, a): return rng.permutation(np.concatenate([a, rng.choice(a, T - len(a))]))
def lists(rng, how):
    O = np.stack([among(rng, np.arange(N)) for g in G])
    if how == "away": O = np.stack([among(rng, [r for r in range(N) if r not in g]) for g in G])
    if how == "home": O = np.stack([among(rng, g) for g in G])
    J = rng.integers(0, R, (H, T)); J[:, rng.integers(T)] = rng.permutation(R)[:H]
    if how == "distinct": O[:], J = rng.integers(N), rng.permutation(R)[:H * T].reshape(H, T)
    if how == "hotrank":
        s = rng.integers(1, H); O[:] = np.array([rng.choice(G[(k + s) % H]) for k in range(H)])[:, None]; J = np.stack([rng.permutation(R)[:T] for g in G])
    I = R * O + J
    if how == "edge":
        C, Q = rng.integers(0, 2 * N, (H, T)), rng.permutation(T)
        C[:, Q[:2 * N]] = np.stack([rng.permutation(2 * N) for g in G]); C[:, Q[2 * N]] = rng.permutation(2 * N)[:H]
        I = R * (C // 2) + (R - 1) * (C % 2)
    return {"idx": np.stack([pack(I[K[r]], 16) for r in range(N)])}
def setup_inputs(rng):
    return dict({"tab": rng.standard_normal((N, 128, R), dtype=np.float32).astype(ml_dtypes.bfloat16)}, **lists(rng, "uniform"))
def setup_inputs_away(rng):
    d = setup_inputs(rng); d.update(lists(rng, "away"))
    for k in ("tab",): d[k] = (d[k].astype(np.float32) * 1048576.0).astype(d[k].dtype)
    return d
def setup_inputs_distinct(rng):
    d = setup_inputs(rng); d.update(lists(rng, "distinct"))
    for k in ("tab",): d[k] = (d[k].astype(np.float32) * (1 / 1024.0)).astype(d[k].dtype)
    return d
def setup_inputs_edge(rng):
    d = setup_inputs(rng); d.update(lists(rng, "edge"))
    return d
def setup_inputs_home(rng):
    d = setup_inputs(rng); d.update(lists(rng, "home"))
    return d
def setup_inputs_hotrank(rng):
    d = setup_inputs(rng); d.update(lists(rng, "hotrank"))
    return d
def check_inputs(x):
    bad = []
    if x["idx"].min() < 0 or x["idx"].max() >= N * R: bad.append("idx out of range")
    if any((x["idx"][r] != x["idx"][s]).any() for r in range(N) for s in range(r) if HOST[r] == HOST[s]): bad.append("two ranks of one host hold different lists")
    return bad
def reference(tab, idx):
    A = np.concatenate(list(tab), axis=1)
    return {"y": np.stack([A[:, entries(idx[r])] for r in range(N)])}

@@ -1,0 +1,291 @@
+from concourse.bass import DstId, RemoteDMATransfer
+from concourse.mybir import AluOpType, ActivationFunctionType
+
+PART = 8192
+BLK = 512
+GRP = 16
+LC = 64
+BC = LC // 2
+FIRST = 64
+OWN, M, P, D = 0, 1, 2, 3
+
+SCRATCH = {
+    "tabs": ("sbuf", [128, PART], "bfloat16"),
+    "lists": ("sbuf", [128, 4 * LC], "int32"),
+    "off": ("sbuf", [128, 4 * LC], "uint16"),
+    "got": ("sbuf", [128, 4 * 2 * BLK], "bfloat16"),
+    "win0": ("sbuf", [128, 4 * BLK], "bfloat16"),
+    "win1": ("sbuf", [128, 4 * BLK], "bfloat16"),
+    "pick": ("sbuf", [128, LC], "uint16"),
+    "res": ("sbuf", [128, 2 * BLK], "bfloat16"),
+    "lane": ("sbuf", [128, LC], "int32"),
+    "col": ("sbuf", [128, LC], "int32"),
+    "term": ("sbuf", [128, 6 * LC], "int32"),
+}
+SEMAPHORES = ["idx", "tab", "sent", "iot", "lr", "lm", "lp", "ld", "vec", "gd", "gm", "gp", "go",
+              "ra", "sel", "w0", "w1", "c0", "c1", "st0", "st1", "left"]
+
+
+def hosts_of(T, topo):
+    ranks = {}
+    for c in T.cores:
+        ranks.setdefault(topo.host(c), []).append(c)
+    near = {}
+    for h in ranks:
+        near[h] = {}
+        for x in ranks:
+            if x == h:
+                continue
+            if topo.rack(x) == topo.rack(h):
+                near[h]["m"] = x
+            elif topo.may_write(ranks[h][0], ranks[x][0]):
+                near[h]["p"] = x
+            else:
+                near[h]["d"] = x
+    return ranks, near
+
+
+def relays_of(ranks, topo):
+    a = ranks[0]
+    chip = [c for c in range(a - 127 if a > 127 else 0, a + 128) if (topo.host(c), topo.chip(c)) == (topo.host(a), topo.chip(a))]
+    free = [c for c in chip if c not in ranks]
+    same = [c for c in free if topo.die(c) == topo.die(a)]
+    other = [c for c in free if topo.die(c) != topo.die(a)]
+    return {"M0": same[-1], "M1": other[1], "P0": other[0], "P1": other[2]}
+
+
+def steps_of(slots):
+    cur, out = 0, []
+    for o, s in enumerate(slots):
+        if s is not None and s != cur:
+            out.append((o, s - cur))
+            cur = s
+    return out
+
+
+def engines(mask, part, parts):
+    e = [i for i in range(mask.bit_length()) if (mask >> i) & 1]
+    n = len(e) // parts
+    return sum(1 << i for i in e[part * n:(part + 1) * n])
+
+
+def count(mask):
+    return bin(mask).count("1")
+
+
+def rank_program(g, core, T, topo):
+    ranks, near = hosts_of(T, topo)
+    h = topo.host(core)
+    if h not in ranks or topo.chip(core) != topo.chip(ranks[h][0]):
+        return
+    relay = {x: relays_of(ranks[x], topo) for x in ranks}
+    role = [k for k in relay[h] if relay[h][k] == core]
+    rank = T.rank_of(core)
+    if rank is None and not role:
+        return
+    m, p, d = near[h]["m"], near[h]["p"], near[h]["d"]
+    s = T.sem
+    V, S = g.vector, g.scalar
+    win = [T.win0, T.win1]
+    nranks = len(T.cores)
+    nvec = [0]
+    nleft = [0]
+
+    def vec(ins):
+        ins.then_inc(s.vec, 1)
+        nvec[0] += 1
+
+    def vec_done():
+        V.wait_ge(s.vec, nvec[0])
+
+    def to(dst, mask, sem, src, dest):
+        rid, pid = topo.addr(dst, core)
+        nleft[0] += count(mask)
+        return RemoteDMATransfer(dst_ids=[DstId(rid=rid, pnc=pid)], dma_engine_mask=mask, remote_sem=sem, src=src, dst=dest)
+
+    off_chip = topo.mask(core, ranks[m][0])
+    mate = [c for c in ranks[h] if c != core][0]
+    on_chip = topo.mask(core, mate)
+    inner = on_chip & ~off_chip
+
+    def slot(k, n=1):
+        return slice(k * BLK, (k + n) * BLK)
+
+    def rank_slots(x, blk):
+        src, own = {}, []
+        for o in range(nranks):
+            ho = topo.host(T.cores[o])
+            if ho == x:
+                k = o
+            elif ho == near[x]["m"]:
+                k = "m"
+            elif ho == near[x]["p"]:
+                k = "p"
+            else:
+                k = "p" if blk else "m"
+            own.append(src.setdefault(k, len(src)))
+        return src, own
+
+    def relay_slots(x, name):
+        hs = [x]
+        if name == "M0":
+            hs.append(near[x]["p"])
+        if name == "P1":
+            hs.append(near[x]["m"])
+        care = [o for o in range(nranks) if topo.host(T.cores[o]) in hs]
+        return {o: k for k, o in enumerate(care)}
+
+    def picks(lists, steps, width):
+        n = max(len(x) for x in steps)
+        V.wait_ge(s.iot, 2)
+        for b in range(len(steps)):
+            for i in range(n):
+                o, dl = steps[b][i] if i < len(steps[b]) else (0, 0)
+                vec(V.tensor_scalar(T.term[:, i * LC + b * BC:i * LC + (b + 1) * BC], lists[b], o * PART, dl * BLK,
+                                    AluOpType.is_ge, AluOpType.mult))
+        vec(V.tensor_scalar(T.term[:, n * LC:n * LC + width], T.lane[:, 0:width], GRP - 1, None, AluOpType.bitwise_and))
+        vec_done()
+        terms = [T.term[:, i * LC:i * LC + width] for i in range(n + 1)] + [T.col[:, 0:width]]
+        while len(terms) > 1:
+            rest = []
+            for i in range(0, len(terms), 2):
+                if i + 1 < len(terms):
+                    vec(V.tensor_tensor(terms[i], terms[i], terms[i + 1], AluOpType.add))
+                rest.append(terms[i])
+            if len(rest) > 1 and len(terms) % 2:
+                rest = rest[:-1] + [terms[-1]]
+            vec_done()
+            terms = rest
+        vec(V.tensor_copy(T.pick[:, 0:width], terms[0]))
+        return nvec[0]
+
+    g.iota(T.lane[:], [[0, LC]], 0, 1).then_inc(s.iot, 1)
+    g.iota(T.col[:], [[0, 2], [GRP, BC]], 0, 0).then_inc(s.iot, 1)
+
+    if role:
+        name = role[0]
+        blk = int(name[1])
+        target = m if name[0] == "M" else p
+        mine = relay_slots(h, name)
+        width = len(mine) * BLK
+        g.wait_ge(s.lr, count(engines(off_chip, 0, 2)))
+        lst = T.lists[:, 0:LC]
+        if blk == 0:
+            place, sem = (M, s.lm) if name[0] == "M" else (P, s.lp)
+            there = T.lists[:, place * LC:(place + 1) * LC]
+            g.remote_dma_fused([to(c, engines(on_chip, i, 2), sem, lst, there) for i, c in enumerate(ranks[h])], local_sem=s.left)
+        else:
+            there = T.lists[:, D * LC:(D + 1) * LC]
+            c = ranks[p][1] if name[0] == "M" else ranks[m][0]
+            g.remote_dma_fused([to(c, off_chip, s.ld, lst, there)], local_sem=s.left)
+        V.wait_ge(s.lr, count(engines(off_chip, 0, 2)))
+        own = [mine.get(o) for o in range(nranks)]
+        ready = picks([T.lists[:, blk * BC:(blk + 1) * BC]], [steps_of(own)], BC)
+        need = 2 * count(engines(inner, 0, 2)) + (len(mine) - 2) * count(engines(off_chip, 0, 2))
+        half = BC // 2
+        V.wait_ge(s.vec, ready)
+        V.wait_ge(s.ra, need)
+        V.tensor_copy(T.res[:, 0:BLK // 2], T.win0[:, 0:width].indirect(T.pick[:, 0:half])).then_inc(s.sel, 1)
+        S.wait_ge(s.vec, ready)
+        S.wait_ge(s.ra, need)
+        S.activation(T.res[:, BLK // 2:BLK], T.win0[:, 0:width].indirect(T.pick[:, half:BC]),
+                     ActivationFunctionType.Copy, bias=-0.0).then_inc(s.sel, 1)
+        src, _ = rank_slots(target, blk)
+        k = src["m" if name[0] == "M" else "p"]
+        sem = s.w1 if blk else s.w0
+        g.wait_ge(s.sel, 2)
+        g.remote_dma_fused([to(c, engines(off_chip, i, 2), sem, T.res[:, 0:BLK], win[blk][:, slot(k)])
+                            for i, c in enumerate(ranks[target])], local_sem=s.left)
+        g.wait_ge(s.left, nleft[0])
+        return
+
+    me = ranks[h].index(core)
+    for k in range(128 // GRP):
+        q = g.sync if k % 2 == 0 else S
+        q.dma_start(T.lists[k * GRP:(k + 1) * GRP, 0:LC], T.idx[:]).then_inc(s.idx, 16)
+    nidx = 16 * (128 // GRP)
+    g.sync.dma_start(T.tabs[0:FIRST, :], T.tab[0:FIRST, :]).then_inc(s.tab, 16)
+    g.sync.wait_ge(s.sent, 1)
+    g.sync.dma_start(T.tabs[FIRST:128, :], T.tab[FIRST:128, :]).then_inc(s.tab, 16)
+    g.wait_ge(s.idx, nidx)
+    rel = [relay[m]["M0"], relay[m]["M1"]] if me == 0 else [relay[p]["P0"], relay[p]["P1"]]
+    g.remote_dma_fused([to(c, engines(off_chip, i, 2), s.lr, T.lists[:, 0:LC], T.lists[:, 0:LC]) for i, c in enumerate(rel)],
+                       local_sem=s.left)
+    g.sem_inc(s.sent, 1)
+
+    def offsets(place):
+        vec(V.tensor_scalar(T.off[:, place * LC:(place + 1) * LC], T.lists[:, place * LC:(place + 1) * LC],
+                            rank * PART, PART - 1, AluOpType.subtract, AluOpType.min))
+        return nvec[0]
+
+    slots = [rank_slots(h, b) for b in range(2)]
+    V.wait_ge(s.idx, nidx)
+    ready = {OWN: offsets(OWN)}
+    picked = picks([T.lists[:, b * BC:(b + 1) * BC] for b in range(2)], [steps_of(slots[b][1]) for b in range(2)], LC)
+
+    def landing(place, b):
+        if place == OWN:
+            return win[b][:, slot(slots[b][0][rank])]
+        return T.got[:, slot(2 * place + b)]
+
+    arrive = {M: s.lm, P: s.lp, D: s.ld}
+    listed = {M: count(engines(on_chip, 0, 2)), P: count(engines(on_chip, 0, 2)), D: count(off_chip)}
+    gsem = {OWN: s.go, M: s.gm, P: s.gp, D: s.gd}
+
+    def conv(place):
+        V.wait_ge(arrive[place], listed[place])
+        ready[place] = offsets(place)
+
+    def gather(place):
+        offs = [T.off[:, place * LC + b * BC:place * LC + (b + 1) * BC] for b in range(2)]
+        V.wait_ge(s.vec, ready[place])
+        V.tensor_copy(landing(place, 0), T.tabs[:, 0:PART].indirect(offs[0])).then_inc(gsem[place], 1)
+        S.wait_ge(s.vec, ready[place])
+        S.activation(landing(place, 1), T.tabs[:, 0:PART].indirect(offs[1]), ActivationFunctionType.Copy,
+                     bias=-0.0).then_inc(gsem[place], 1)
+
+    conv(D)
+    conv(M)
+    V.wait_ge(s.tab, 32)
+    S.wait_ge(s.tab, 32)
+    gather(D)
+    conv(P)
+    gather(M)
+    gather(P)
+    gather(OWN)
+
+    g.wait_ge(s.gd, 2)
+    tr = []
+    for i, (c, x, name) in enumerate([(relay[p]["M0"], p, "M0"), (relay[m]["P1"], m, "P1")]):
+        k = relay_slots(x, name)[rank]
+        tr.append(to(c, engines(off_chip, i, 2), s.ra, landing(D, i), T.win0[:, slot(k)]))
+    g.remote_dma_fused(tr, local_sem=s.left)
+    for place, sem, x in ((M, s.gm, "M"), (P, s.gp, "P")):
+        g.wait_ge(sem, 2)
+        tr = []
+        for i in range(2):
+            name = x + str(i)
+            k = relay_slots(h, name)[rank]
+            tr.append(to(relay[h][name], engines(inner, i, 2), s.ra, landing(place, i), T.win0[:, slot(k)]))
+        g.remote_dma_fused(tr, local_sem=s.left)
+    g.wait_ge(s.go, 2)
+    g.remote_dma_fused([to(mate, engines(on_chip, b, 2), s.w1 if b else s.w0, landing(OWN, b), landing(OWN, b)) for b in range(2)],
+                       local_sem=s.left)
+
+    need = count(engines(on_chip, 0, 2)) + 2 * count(engines(off_chip, 0, 2))
+    V.wait_ge(s.vec, picked)
+    V.wait_ge(s.go, 2)
+    V.wait_ge(s.w0, need)
+    V.tensor_copy(T.res[:, 0:BLK], T.win0[:, 0:4 * BLK].indirect(T.pick[:, 0:BC])).then_inc(s.c0, 1)
+    g.sync.wait_ge(s.c0, 1)
+    g.sync.dma_start(T.y[:, 0:BLK], T.res[:, 0:BLK]).then_inc(s.st0, 16)
+    g.sync.wait_ge(s.st0, 16)
+    S.wait_ge(s.vec, picked)
+    S.wait_ge(s.go, 2)
+    S.wait_ge(s.w1, need)
+    S.activation(T.res[:, BLK:2 * BLK], T.win1[:, 0:4 * BLK].indirect(T.pick[:, BC:LC]), ActivationFunctionType.Copy,
+                 bias=-0.0).then_inc(s.c1, 1)
+    S.wait_ge(s.c1, 1)
+    S.dma_start(T.y[:, BLK:2 * BLK], T.res[:, BLK:2 * BLK]).then_inc(s.st1, 16)
+    S.wait_ge(s.st1, 16)
+    g.wait_ge(s.left, nleft[0])

@@ -3,14 +3,19 @@ from concourse.mybir import AluOpType, ActivationFunctionType
 
 PART = 8192
 BLK = 512
+HALF = BLK // 2
 GRP = 16
 LC = 64
 BC = LC // 2
-FIRST = 64
+QC = LC // 4
+CHUNK = 64
 OWN, M, P, D = 0, 1, 2, 3
+
+RELAYS = {"Ma": ("m", 0, True), "Mc": ("m", 1, False), "Pa": ("p", 1, True), "Pc": ("p", 0, False)}
 
 SCRATCH = {
     "tabs": ("sbuf", [128, PART], "bfloat16"),
+    "ldram": ("dram", [128, LC], "int32"),
     "lists": ("sbuf", [128, 4 * LC], "int32"),
     "off": ("sbuf", [128, 4 * LC], "uint16"),
     "got": ("sbuf", [128, 4 * 2 * BLK], "bfloat16"),
@@ -20,10 +25,11 @@ SCRATCH = {
     "res": ("sbuf", [128, 2 * BLK], "bfloat16"),
     "lane": ("sbuf", [128, LC], "int32"),
     "col": ("sbuf", [128, LC], "int32"),
-    "term": ("sbuf", [128, 6 * LC], "int32"),
+    "term": ("sbuf", [128, 8 * LC], "int32"),
 }
-SEMAPHORES = ["idx", "tab", "sent", "iot", "lr", "lm", "lp", "ld", "vec", "gd", "gm", "gp", "go",
-              "ra", "sel", "w0", "w1", "c0", "c1", "st0", "st1", "left"]
+SEMAPHORES = (["idx", "own", "iot", "lr", "sent", "lm", "lp", "ld", "vec", "tab", "ra", "left"]
+              + [k + str(b) for k in ("rd", "sel", "st", "w") for b in range(2)]
+              + [k + str(b) + str(q) for k in "xc" for b in range(2) for q in range(2)] + ["g%d" % k for k in range(5)])
 
 
 def hosts_of(T, topo):
@@ -51,12 +57,12 @@ def relays_of(ranks, topo):
     free = [c for c in chip if c not in ranks]
     same = [c for c in free if topo.die(c) == topo.die(a)]
     other = [c for c in free if topo.die(c) != topo.die(a)]
-    return {"M0": same[-1], "M1": other[1], "P0": other[0], "P1": other[2]}
+    return {"Ma": same[0], "Pa": same[1], "Pc": other[2], "Mc": other[3]}
 
 
-def steps_of(slots):
+def steps_of(bases):
     cur, out = 0, []
-    for o, s in enumerate(slots):
+    for o, s in enumerate(bases):
         if s is not None and s != cur:
             out.append((o, s - cur))
             cur = s
@@ -83,11 +89,11 @@ def rank_program(g, core, T, topo):
     rank = T.rank_of(core)
     if rank is None and not role:
         return
-    m, p, d = near[h]["m"], near[h]["p"], near[h]["d"]
+    m, p = near[h]["m"], near[h]["p"]
     s = T.sem
     V, S = g.vector, g.scalar
     win = [T.win0, T.win1]
-    nranks = len(T.cores)
+    owners = [topo.host(c) for c in T.cores]
     nvec = [0]
     nleft = [0]
 
@@ -103,45 +109,47 @@ def rank_program(g, core, T, topo):
         nleft[0] += count(mask)
         return RemoteDMATransfer(dst_ids=[DstId(rid=rid, pnc=pid)], dma_engine_mask=mask, remote_sem=sem, src=src, dst=dest)
 
+    def send(tr):
+        g.remote_dma_fused(tr, local_sem=s.left)
+
     off_chip = topo.mask(core, ranks[m][0])
     mate = [c for c in ranks[h] if c != core][0]
     on_chip = topo.mask(core, mate)
     inner = on_chip & ~off_chip
+    off2 = [engines(off_chip, i, 2) for i in range(2)]
+    in2 = [engines(inner, i, 2) for i in range(2)]
+    feed_mask = {"Pc": in2[0], "Mc": in2[1], "Ma": off2[0], "Pa": inner}
 
-    def slot(k, n=1):
-        return slice(k * BLK, (k + n) * BLK)
+    def whole(k):
+        return slice(HALF + k * BLK, HALF + (k + 1) * BLK)
 
-    def rank_slots(x, blk):
-        src, own = {}, []
-        for o in range(nranks):
-            ho = topo.host(T.cores[o])
-            if ho == x:
-                k = o
-            elif ho == near[x]["m"]:
-                k = "m"
-            elif ho == near[x]["p"]:
-                k = "p"
-            else:
-                k = "p" if blk else "m"
-            own.append(src.setdefault(k, len(src)))
-        return src, own
+    def half(q):
+        return slice(0, HALF) if q else slice(4 * BLK - HALF, 4 * BLK)
 
-    def relay_slots(x, name):
-        hs = [x]
-        if name == "M0":
-            hs.append(near[x]["p"])
-        if name == "P1":
-            hs.append(near[x]["m"])
-        care = [o for o in range(nranks) if topo.host(T.cores[o]) in hs]
-        return {o: k for k, o in enumerate(care)}
+    def view(q):
+        return slice(0, 4 * BLK - HALF) if q else slice(HALF, 4 * BLK)
 
-    def picks(lists, steps, width):
-        n = max(len(x) for x in steps)
+    def relay_whole(k):
+        return slice(BLK + k * BLK, 2 * BLK + k * BLK)
+
+    def relay_half(q, k):
+        at = (0 if q else 3 * BLK) + k * HALF
+        return slice(at, at + HALF)
+
+    def nth(x, o):
+        return ranks[x].index(T.cores[o])
+
+    def picks(pieces, w):
+        pieces = [(c, steps_of(x)) for c, x in pieces]
+        n = max(len(x) for _, x in pieces)
+        width = w * len(pieces)
+        g.iota(T.lane[:], [[0, LC]], 0, 1).then_inc(s.iot, 1)
+        g.iota(T.col[:], [[0, LC // w], [GRP, w]], 0, 0).then_inc(s.iot, 1)
         V.wait_ge(s.iot, 2)
-        for b in range(len(steps)):
+        for k, (c, steps) in enumerate(pieces):
             for i in range(n):
-                o, dl = steps[b][i] if i < len(steps[b]) else (0, 0)
-                vec(V.tensor_scalar(T.term[:, i * LC + b * BC:i * LC + (b + 1) * BC], lists[b], o * PART, dl * BLK,
+                o, dl = steps[i] if i < len(steps) else (0, 0)
+                vec(V.tensor_scalar(T.term[:, i * LC + k * w:i * LC + (k + 1) * w], T.lists[:, c:c + w], o * PART, dl,
                                     AluOpType.is_ge, AluOpType.mult))
         vec(V.tensor_scalar(T.term[:, n * LC:n * LC + width], T.lane[:, 0:width], GRP - 1, None, AluOpType.bitwise_and))
         vec_done()
@@ -152,140 +160,140 @@ def rank_program(g, core, T, topo):
                 if i + 1 < len(terms):
                     vec(V.tensor_tensor(terms[i], terms[i], terms[i + 1], AluOpType.add))
                 rest.append(terms[i])
-            if len(rest) > 1 and len(terms) % 2:
-                rest = rest[:-1] + [terms[-1]]
             vec_done()
             terms = rest
         vec(V.tensor_copy(T.pick[:, 0:width], terms[0]))
         return nvec[0]
 
-    g.iota(T.lane[:], [[0, LC]], 0, 1).then_inc(s.iot, 1)
-    g.iota(T.col[:], [[0, 2], [GRP, BC]], 0, 0).then_inc(s.iot, 1)
+    def copy(Q, dest, src, sem):
+        if Q is V:
+            V.tensor_copy(dest, src).then_inc(sem, 1)
+        else:
+            S.activation(dest, src, ActivationFunctionType.Copy, bias=-0.0).then_inc(sem, 1)
 
     if role:
         name = role[0]
-        blk = int(name[1])
-        target = m if name[0] == "M" else p
-        mine = relay_slots(h, name)
-        width = len(mine) * BLK
-        g.wait_ge(s.lr, count(engines(off_chip, 0, 2)))
-        lst = T.lists[:, 0:LC]
-        if blk == 0:
-            place, sem = (M, s.lm) if name[0] == "M" else (P, s.lp)
-            there = T.lists[:, place * LC:(place + 1) * LC]
-            g.remote_dma_fused([to(c, engines(on_chip, i, 2), sem, lst, there) for i, c in enumerate(ranks[h])], local_sem=s.left)
+        kind, b, diag = RELAYS[name]
+        target, third = (m, p) if kind == "m" else (p, m)
+        nlist = count(off2[0])
+        g.wait_ge(s.lr, nlist)
+        if diag:
+            place, sem = (M, s.lm) if kind == "m" else (P, s.lp)
+            goal = list(zip(ranks[h], off2))
         else:
-            there = T.lists[:, D * LC:(D + 1) * LC]
-            c = ranks[p][1] if name[0] == "M" else ranks[m][0]
-            g.remote_dma_fused([to(c, off_chip, s.ld, lst, there)], local_sem=s.left)
-        V.wait_ge(s.lr, count(engines(off_chip, 0, 2)))
-        own = [mine.get(o) for o in range(nranks)]
-        ready = picks([T.lists[:, blk * BC:(blk + 1) * BC]], [steps_of(own)], BC)
-        need = 2 * count(engines(inner, 0, 2)) + (len(mine) - 2) * count(engines(off_chip, 0, 2))
-        half = BC // 2
-        V.wait_ge(s.vec, ready)
-        V.wait_ge(s.ra, need)
-        V.tensor_copy(T.res[:, 0:BLK // 2], T.win0[:, 0:width].indirect(T.pick[:, 0:half])).then_inc(s.sel, 1)
-        S.wait_ge(s.vec, ready)
-        S.wait_ge(s.ra, need)
-        S.activation(T.res[:, BLK // 2:BLK], T.win0[:, 0:width].indirect(T.pick[:, half:BC]),
-                     ActivationFunctionType.Copy, bias=-0.0).then_inc(s.sel, 1)
-        src, _ = rank_slots(target, blk)
-        k = src["m" if name[0] == "M" else "p"]
-        sem = s.w1 if blk else s.w0
-        g.wait_ge(s.sel, 2)
-        g.remote_dma_fused([to(c, engines(off_chip, i, 2), sem, T.res[:, 0:BLK], win[blk][:, slot(k)])
-                            for i, c in enumerate(ranks[target])], local_sem=s.left)
+            place, sem = D, s.ld
+            goal = [(ranks[p][1] if kind == "m" else ranks[m][0], off_chip)]
+        send([to(c, mask, sem, T.ldram[:], T.lists[:, place * LC:(place + 1) * LC]) for c, mask in goal])
+        g.sync.wait_ge(s.lr, nlist)
+        g.sync.dma_start(T.lists[:, b * BC:(b + 1) * BC], T.ldram[:, b * BC:(b + 1) * BC]).then_inc(s.idx, 16)
+        V.wait_ge(s.idx, 16)
+        if diag:
+            bases = [[(BLK + HALF if q else 0) + nth(h, o) * BLK if x == h else
+                      ((0 if q else 2 * BLK) + nth(third, o) * HALF if x == third else None) for o, x in enumerate(owners)]
+                     for q in range(2)]
+            ready = picks([(b * BC + q * QC, bases[q]) for q in range(2)], QC)
+            views = [T.win0[:, BLK:4 * BLK], T.win0[:, 0:3 * BLK]]
+            goals = [(win[b][:, half(q)], s["x%d%d" % (b, q)]) for q in range(2)]
+        else:
+            ready = picks([(b * BC, [nth(h, o) * BLK if x == h else None for o, x in enumerate(owners)])], BC)
+            views = [T.win0[:, BLK:3 * BLK]]
+            goals = [(win[b][:, whole(2)], s["w%d" % b])]
+        n = BLK // len(views)
+        for Q in (V, S):
+            Q.wait_ge(s.vec, ready)
+            Q.wait_ge(s.ra, 2 * count(feed_mask[name]))
+        for q, (source, (dest, sem)) in enumerate(zip(views, goals)):
+            for i, Q in enumerate((V, S)):
+                if diag:
+                    Q.wait_ge(s["rd%d" % q], 2 * count(off2[0]))
+                o = q * n + i * n // 2
+                copy(Q, T.res[:, o:o + n // 2], source.indirect(T.pick[:, o // GRP:(o + n // 2) // GRP]), s["sel%d" % q])
+            g.wait_ge(s["sel%d" % q], 2)
+            send([to(ranks[target][b], off_chip, sem, T.res[:, q * n:(q + 1) * n], dest)])
         g.wait_ge(s.left, nleft[0])
         return
 
     me = ranks[h].index(core)
     for k in range(128 // GRP):
-        q = g.sync if k % 2 == 0 else S
-        q.dma_start(T.lists[k * GRP:(k + 1) * GRP, 0:LC], T.idx[:]).then_inc(s.idx, 16)
+        Q = g.sync if k % 2 == 0 else S
+        Q.dma_start(T.ldram[k * GRP:(k + 1) * GRP, :], T.idx[:]).then_inc(s.idx, 16)
     nidx = 16 * (128 // GRP)
-    g.sync.dma_start(T.tabs[0:FIRST, :], T.tab[0:FIRST, :]).then_inc(s.tab, 16)
-    g.sync.wait_ge(s.sent, 1)
-    g.sync.dma_start(T.tabs[FIRST:128, :], T.tab[FIRST:128, :]).then_inc(s.tab, 16)
+    ntab = 128 // CHUNK
+    for k in range(ntab):
+        if k == ntab // 2:
+            g.sync.wait_ge(s.sent, 1)
+        g.sync.dma_start(T.tabs[k * CHUNK:(k + 1) * CHUNK, :], T.tab[k * CHUNK:(k + 1) * CHUNK, :]).then_inc(s.tab, 16)
+    g.sync.wait_ge(s.idx, nidx)
+    g.sync.dma_start(T.lists[:, 0:LC], T.ldram[:]).then_inc(s.own, 16)
     g.wait_ge(s.idx, nidx)
-    rel = [relay[m]["M0"], relay[m]["M1"]] if me == 0 else [relay[p]["P0"], relay[p]["P1"]]
-    g.remote_dma_fused([to(c, engines(off_chip, i, 2), s.lr, T.lists[:, 0:LC], T.lists[:, 0:LC]) for i, c in enumerate(rel)],
-                       local_sem=s.left)
+    x, kind = ((m, "M"), (p, "P"))[me]
+    send([to(relay[x][kind + k], mask, s.lr, T.ldram[:], T.ldram[:]) for k, mask in zip("ca", off2)])
     g.sem_inc(s.sent, 1)
 
+    arrive = {OWN: (s.own, 16), M: (s.lm, count(off2[0])), P: (s.lp, count(off2[0])), D: (s.ld, count(off_chip))}
+    ready = {}
+
     def offsets(place):
+        V.wait_ge(*arrive[place])
         vec(V.tensor_scalar(T.off[:, place * LC:(place + 1) * LC], T.lists[:, place * LC:(place + 1) * LC],
                             rank * PART, PART - 1, AluOpType.subtract, AluOpType.min))
-        return nvec[0]
+        ready[place] = nvec[0]
 
-    slots = [rank_slots(h, b) for b in range(2)]
-    V.wait_ge(s.idx, nidx)
-    ready = {OWN: offsets(OWN)}
-    picked = picks([T.lists[:, b * BC:(b + 1) * BC] for b in range(2)], [steps_of(slots[b][1]) for b in range(2)], LC)
+    def got(place, lo, n):
+        return T.got[:, 2 * place * BLK + lo:2 * place * BLK + lo + n]
 
-    def landing(place, b):
-        if place == OWN:
-            return win[b][:, slot(slots[b][0][rank])]
-        return T.got[:, slot(2 * place + b)]
+    def far(name, x, q, mask):
+        lo = RELAYS[name][1] * BLK + q * HALF
+        return (D, lo, HALF, got(D, lo, HALF), relay[x][name], T.win0[:, relay_half(q, me)], s["rd%d" % q], mask)
 
-    arrive = {M: s.lm, P: s.lp, D: s.ld}
-    listed = {M: count(engines(on_chip, 0, 2)), P: count(engines(on_chip, 0, 2)), D: count(off_chip)}
-    gsem = {OWN: s.go, M: s.gm, P: s.gp, D: s.gd}
+    def close(name, place):
+        lo = RELAYS[name][1] * BLK
+        return (place, lo, BLK, got(place, lo, BLK), relay[h][name], T.win0[:, relay_whole(me)], s.ra, feed_mask[name])
 
-    def conv(place):
-        V.wait_ge(arrive[place], listed[place])
-        ready[place] = offsets(place)
+    calls = [[far("Ma", p, q, off2[0]), far("Pa", m, q, off2[1])] for q in range(2)]
+    calls += [[close("Pc", P), close("Mc", M)], [close("Ma", M), close("Pa", P)],
+              [(OWN, b * BLK, BLK, win[b][:, whole(me)], None if b == me else mate, win[b][:, whole(me)], s["w%d" % b], on_chip)
+               for b in range(2)]]
+    for k, call in enumerate(calls):
+        for c in call:
+            if c[0] not in ready:
+                offsets(c[0])
+        if k == 0:
+            V.wait_ge(s.tab, 16 * ntab)
+            S.wait_ge(s.tab, 16 * ntab)
+        for Q, (place, lo, n, where, *_) in zip((V, S), call):
+            Q.wait_ge(s.vec, ready[place])
+            o = place * LC + lo // GRP
+            copy(Q, where, T.tabs[:, 0:PART].indirect(T.off[:, o:o + n // GRP]), s["g%d" % k])
+        g.wait_ge(s["g%d" % k], 2)
+        send([to(c, mask, sem, where, there) for _, _, _, where, c, there, sem, mask in call if c is not None])
 
-    def gather(place):
-        offs = [T.off[:, place * LC + b * BC:place * LC + (b + 1) * BC] for b in range(2)]
-        V.wait_ge(s.vec, ready[place])
-        V.tensor_copy(landing(place, 0), T.tabs[:, 0:PART].indirect(offs[0])).then_inc(gsem[place], 1)
-        S.wait_ge(s.vec, ready[place])
-        S.activation(landing(place, 1), T.tabs[:, 0:PART].indirect(offs[1]), ActivationFunctionType.Copy,
-                     bias=-0.0).then_inc(gsem[place], 1)
+    def bases_of(b, q):
+        slots = [nth(h, o) if x == h else (2 if x == (p, m)[b] else 3) for o, x in enumerate(owners)]
+        return [(0 if k == 3 else (k + 1) * BLK) if q else k * BLK for k in slots]
 
-    conv(D)
-    conv(M)
-    V.wait_ge(s.tab, 32)
-    S.wait_ge(s.tab, 32)
-    gather(D)
-    conv(P)
-    gather(M)
-    gather(P)
-    gather(OWN)
-
-    g.wait_ge(s.gd, 2)
-    tr = []
-    for i, (c, x, name) in enumerate([(relay[p]["M0"], p, "M0"), (relay[m]["P1"], m, "P1")]):
-        k = relay_slots(x, name)[rank]
-        tr.append(to(c, engines(off_chip, i, 2), s.ra, landing(D, i), T.win0[:, slot(k)]))
-    g.remote_dma_fused(tr, local_sem=s.left)
-    for place, sem, x in ((M, s.gm, "M"), (P, s.gp, "P")):
-        g.wait_ge(sem, 2)
-        tr = []
-        for i in range(2):
-            name = x + str(i)
-            k = relay_slots(h, name)[rank]
-            tr.append(to(relay[h][name], engines(inner, i, 2), s.ra, landing(place, i), T.win0[:, slot(k)]))
-        g.remote_dma_fused(tr, local_sem=s.left)
-    g.wait_ge(s.go, 2)
-    g.remote_dma_fused([to(mate, engines(on_chip, b, 2), s.w1 if b else s.w0, landing(OWN, b), landing(OWN, b)) for b in range(2)],
-                       local_sem=s.left)
-
-    need = count(engines(on_chip, 0, 2)) + 2 * count(engines(off_chip, 0, 2))
-    V.wait_ge(s.vec, picked)
-    V.wait_ge(s.go, 2)
-    V.wait_ge(s.w0, need)
-    V.tensor_copy(T.res[:, 0:BLK], T.win0[:, 0:4 * BLK].indirect(T.pick[:, 0:BC])).then_inc(s.c0, 1)
-    g.sync.wait_ge(s.c0, 1)
-    g.sync.dma_start(T.y[:, 0:BLK], T.res[:, 0:BLK]).then_inc(s.st0, 16)
-    g.sync.wait_ge(s.st0, 16)
-    S.wait_ge(s.vec, picked)
-    S.wait_ge(s.go, 2)
-    S.wait_ge(s.w1, need)
-    S.activation(T.res[:, BLK:2 * BLK], T.win1[:, 0:4 * BLK].indirect(T.pick[:, BC:LC]), ActivationFunctionType.Copy,
-                 bias=-0.0).then_inc(s.c1, 1)
-    S.wait_ge(s.c1, 1)
-    S.dma_start(T.y[:, BLK:2 * BLK], T.res[:, BLK:2 * BLK]).then_inc(s.st1, 16)
-    S.wait_ge(s.st1, 16)
+    b = me
+    picked = picks([(b * BC + q * QC, bases_of(b, q)) for q in range(2)], QC)
+    for Q in (V, S):
+        Q.wait_ge(s.vec, picked)
+        Q.wait_ge(s["g%d" % (len(calls) - 1)], 2)
+        Q.wait_ge(s["w%d" % b], count(on_chip) + count(off_chip))
+    for q in range(2):
+        c = s["c%d%d" % (b, q)]
+        for i, Q in enumerate((V, S)):
+            o = q * HALF + i * HALF // 2
+            Q.wait_ge(s["x%d%d" % (b, q)], count(off_chip))
+            copy(Q, T.res[:, b * BLK + o:b * BLK + o + HALF // 2],
+                 win[b][:, view(q)].indirect(T.pick[:, o // GRP:(o + HALF // 2) // GRP]), c)
+        o = b * BLK + q * HALF
+        g.wait_ge(c, 2)
+        send([to(mate, on_chip, s["x%d%d" % (b, q)], T.res[:, o:o + HALF], T.res[:, o:o + HALF])])
+        g.sync.wait_ge(c, 2)
+        g.sync.dma_start(T.y[:, o:o + HALF], T.res[:, o:o + HALF]).then_inc(s.st0, 16)
+    for q in range(2):
+        o = (1 - b) * BLK + q * HALF
+        S.wait_ge(s["x%d%d" % (1 - b, q)], count(on_chip))
+        S.dma_start(T.y[:, o:o + HALF], T.res[:, o:o + HALF]).then_inc(s.st1, 16)
+    S.wait_ge(s.st1, 32)
+    g.sync.wait_ge(s.st0, 32)
     g.wait_ge(s.left, nleft[0])

from concourse.bass import DstId, RemoteDMATransfer
from concourse.mybir import AluOpType, ActivationFunctionType

PART = 8192
BLK = 512
HALF = BLK // 2
GRP = 16
LC = 64
BC = LC // 2
QC = LC // 4
CHUNK = 64
OWN, M, P, D = 0, 1, 2, 3

RELAYS = {"Ma": ("m", 0, True), "Mc": ("m", 1, False), "Pa": ("p", 1, True), "Pc": ("p", 0, False)}

SCRATCH = {
    "tabs": ("sbuf", [128, PART], "bfloat16"),
    "ldram": ("dram", [128, LC], "int32"),
    "lists": ("sbuf", [128, 4 * LC], "int32"),
    "off": ("sbuf", [128, 4 * LC], "uint16"),
    "got": ("sbuf", [128, 4 * 2 * BLK], "bfloat16"),
    "win0": ("sbuf", [128, 4 * BLK], "bfloat16"),
    "win1": ("sbuf", [128, 4 * BLK], "bfloat16"),
    "pick": ("sbuf", [128, LC], "uint16"),
    "res": ("sbuf", [128, 2 * BLK], "bfloat16"),
    "lane": ("sbuf", [128, LC], "int32"),
    "col": ("sbuf", [128, LC], "int32"),
    "term": ("sbuf", [128, 8 * LC], "int32"),
}
SEMAPHORES = (["idx", "own", "iot", "lr", "sent", "lm", "lp", "ld", "vec", "tab", "ra", "left"]
              + [k + str(b) for k in ("rd", "sel", "st", "w") for b in range(2)]
              + [k + str(b) + str(q) for k in "xc" for b in range(2) for q in range(2)] + ["g%d" % k for k in range(5)])


def hosts_of(T, topo):
    ranks = {}
    for c in T.cores:
        ranks.setdefault(topo.host(c), []).append(c)
    near = {}
    for h in ranks:
        near[h] = {}
        for x in ranks:
            if x == h:
                continue
            if topo.rack(x) == topo.rack(h):
                near[h]["m"] = x
            elif topo.may_write(ranks[h][0], ranks[x][0]):
                near[h]["p"] = x
            else:
                near[h]["d"] = x
    return ranks, near


def relays_of(ranks, topo):
    a = ranks[0]
    chip = [c for c in range(a - 127 if a > 127 else 0, a + 128) if (topo.host(c), topo.chip(c)) == (topo.host(a), topo.chip(a))]
    free = [c for c in chip if c not in ranks]
    same = [c for c in free if topo.die(c) == topo.die(a)]
    other = [c for c in free if topo.die(c) != topo.die(a)]
    return {"Ma": same[0], "Pa": same[1], "Pc": other[2], "Mc": other[3]}


def steps_of(bases):
    cur, out = 0, []
    for o, s in enumerate(bases):
        if s is not None and s != cur:
            out.append((o, s - cur))
            cur = s
    return out


def engines(mask, part, parts):
    e = [i for i in range(mask.bit_length()) if (mask >> i) & 1]
    n = len(e) // parts
    return sum(1 << i for i in e[part * n:(part + 1) * n])


def count(mask):
    return bin(mask).count("1")


def rank_program(g, core, T, topo):
    ranks, near = hosts_of(T, topo)
    h = topo.host(core)
    if h not in ranks or topo.chip(core) != topo.chip(ranks[h][0]):
        return
    relay = {x: relays_of(ranks[x], topo) for x in ranks}
    role = [k for k in relay[h] if relay[h][k] == core]
    rank = T.rank_of(core)
    if rank is None and not role:
        return
    m, p = near[h]["m"], near[h]["p"]
    s = T.sem
    V, S = g.vector, g.scalar
    win = [T.win0, T.win1]
    owners = [topo.host(c) for c in T.cores]
    nvec = [0]
    nleft = [0]

    def vec(ins):
        ins.then_inc(s.vec, 1)
        nvec[0] += 1

    def vec_done():
        V.wait_ge(s.vec, nvec[0])

    def to(dst, mask, sem, src, dest):
        rid, pid = topo.addr(dst, core)
        nleft[0] += count(mask)
        return RemoteDMATransfer(dst_ids=[DstId(rid=rid, pnc=pid)], dma_engine_mask=mask, remote_sem=sem, src=src, dst=dest)

    def send(tr):
        g.remote_dma_fused(tr, local_sem=s.left)

    off_chip = topo.mask(core, ranks[m][0])
    mate = [c for c in ranks[h] if c != core][0]
    on_chip = topo.mask(core, mate)
    inner = on_chip & ~off_chip
    off2 = [engines(off_chip, i, 2) for i in range(2)]
    in2 = [engines(inner, i, 2) for i in range(2)]
    feed_mask = {"Pc": in2[0], "Mc": in2[1], "Ma": off2[0], "Pa": inner}

    def whole(k):
        return slice(HALF + k * BLK, HALF + (k + 1) * BLK)

    def half(q):
        return slice(0, HALF) if q else slice(4 * BLK - HALF, 4 * BLK)

    def view(q):
        return slice(0, 4 * BLK - HALF) if q else slice(HALF, 4 * BLK)

    def relay_whole(k):
        return slice(BLK + k * BLK, 2 * BLK + k * BLK)

    def relay_half(q, k):
        at = (0 if q else 3 * BLK) + k * HALF
        return slice(at, at + HALF)

    def nth(x, o):
        return ranks[x].index(T.cores[o])

    def picks(pieces, w):
        pieces = [(c, steps_of(x)) for c, x in pieces]
        n = max(len(x) for _, x in pieces)
        width = w * len(pieces)
        g.iota(T.lane[:], [[0, LC]], 0, 1).then_inc(s.iot, 1)
        g.iota(T.col[:], [[0, LC // w], [GRP, w]], 0, 0).then_inc(s.iot, 1)
        V.wait_ge(s.iot, 2)
        for k, (c, steps) in enumerate(pieces):
            for i in range(n):
                o, dl = steps[i] if i < len(steps) else (0, 0)
                vec(V.tensor_scalar(T.term[:, i * LC + k * w:i * LC + (k + 1) * w], T.lists[:, c:c + w], o * PART, dl,
                                    AluOpType.is_ge, AluOpType.mult))
        vec(V.tensor_scalar(T.term[:, n * LC:n * LC + width], T.lane[:, 0:width], GRP - 1, None, AluOpType.bitwise_and))
        vec_done()
        terms = [T.term[:, i * LC:i * LC + width] for i in range(n + 1)] + [T.col[:, 0:width]]
        while len(terms) > 1:
            rest = []
            for i in range(0, len(terms), 2):
                if i + 1 < len(terms):
                    vec(V.tensor_tensor(terms[i], terms[i], terms[i + 1], AluOpType.add))
                rest.append(terms[i])
            vec_done()
            terms = rest
        vec(V.tensor_copy(T.pick[:, 0:width], terms[0]))
        return nvec[0]

    def copy(Q, dest, src, sem):
        if Q is V:
            V.tensor_copy(dest, src).then_inc(sem, 1)
        else:
            S.activation(dest, src, ActivationFunctionType.Copy, bias=-0.0).then_inc(sem, 1)

    if role:
        name = role[0]
        kind, b, diag = RELAYS[name]
        target, third = (m, p) if kind == "m" else (p, m)
        nlist = count(off2[0])
        g.wait_ge(s.lr, nlist)
        if diag:
            place, sem = (M, s.lm) if kind == "m" else (P, s.lp)
            goal = list(zip(ranks[h], off2))
        else:
            place, sem = D, s.ld
            goal = [(ranks[p][1] if kind == "m" else ranks[m][0], off_chip)]
        send([to(c, mask, sem, T.ldram[:], T.lists[:, place * LC:(place + 1) * LC]) for c, mask in goal])
        g.sync.wait_ge(s.lr, nlist)
        g.sync.dma_start(T.lists[:, b * BC:(b + 1) * BC], T.ldram[:, b * BC:(b + 1) * BC]).then_inc(s.idx, 16)
        V.wait_ge(s.idx, 16)
        if diag:
            bases = [[(BLK + HALF if q else 0) + nth(h, o) * BLK if x == h else
                      ((0 if q else 2 * BLK) + nth(third, o) * HALF if x == third else None) for o, x in enumerate(owners)]
                     for q in range(2)]
            ready = picks([(b * BC + q * QC, bases[q]) for q in range(2)], QC)
            views = [T.win0[:, BLK:4 * BLK], T.win0[:, 0:3 * BLK]]
            goals = [(win[b][:, half(q)], s["x%d%d" % (b, q)]) for q in range(2)]
        else:
            ready = picks([(b * BC, [nth(h, o) * BLK if x == h else None for o, x in enumerate(owners)])], BC)
            views = [T.win0[:, BLK:3 * BLK]]
            goals = [(win[b][:, whole(2)], s["w%d" % b])]
        n = BLK // len(views)
        for Q in (V, S):
            Q.wait_ge(s.vec, ready)
            Q.wait_ge(s.ra, 2 * count(feed_mask[name]))
        for q, (source, (dest, sem)) in enumerate(zip(views, goals)):
            for i, Q in enumerate((V, S)):
                if diag:
                    Q.wait_ge(s["rd%d" % q], 2 * count(off2[0]))
                o = q * n + i * n // 2
                copy(Q, T.res[:, o:o + n // 2], source.indirect(T.pick[:, o // GRP:(o + n // 2) // GRP]), s["sel%d" % q])
            g.wait_ge(s["sel%d" % q], 2)
            send([to(ranks[target][b], off_chip, sem, T.res[:, q * n:(q + 1) * n], dest)])
        g.wait_ge(s.left, nleft[0])
        return

    me = ranks[h].index(core)
    for k in range(128 // GRP):
        Q = g.sync if k % 2 == 0 else S
        Q.dma_start(T.ldram[k * GRP:(k + 1) * GRP, :], T.idx[:]).then_inc(s.idx, 16)
    nidx = 16 * (128 // GRP)
    ntab = 128 // CHUNK
    for k in range(ntab):
        if k == ntab // 2:
            g.sync.wait_ge(s.sent, 1)
        g.sync.dma_start(T.tabs[k * CHUNK:(k + 1) * CHUNK, :], T.tab[k * CHUNK:(k + 1) * CHUNK, :]).then_inc(s.tab, 16)
    g.sync.wait_ge(s.idx, nidx)
    g.sync.dma_start(T.lists[:, 0:LC], T.ldram[:]).then_inc(s.own, 16)
    g.wait_ge(s.idx, nidx)
    x, kind = ((m, "M"), (p, "P"))[me]
    send([to(relay[x][kind + k], mask, s.lr, T.ldram[:], T.ldram[:]) for k, mask in zip("ca", off2)])
    g.sem_inc(s.sent, 1)

    arrive = {OWN: (s.own, 16), M: (s.lm, count(off2[0])), P: (s.lp, count(off2[0])), D: (s.ld, count(off_chip))}
    ready = {}

    def offsets(place):
        V.wait_ge(*arrive[place])
        vec(V.tensor_scalar(T.off[:, place * LC:(place + 1) * LC], T.lists[:, place * LC:(place + 1) * LC],
                            rank * PART, PART - 1, AluOpType.subtract, AluOpType.min))
        ready[place] = nvec[0]

    def got(place, lo, n):
        return T.got[:, 2 * place * BLK + lo:2 * place * BLK + lo + n]

    def far(name, x, q, mask):
        lo = RELAYS[name][1] * BLK + q * HALF
        return (D, lo, HALF, got(D, lo, HALF), relay[x][name], T.win0[:, relay_half(q, me)], s["rd%d" % q], mask)

    def close(name, place):
        lo = RELAYS[name][1] * BLK
        return (place, lo, BLK, got(place, lo, BLK), relay[h][name], T.win0[:, relay_whole(me)], s.ra, feed_mask[name])

    calls = [[far("Ma", p, q, off2[0]), far("Pa", m, q, off2[1])] for q in range(2)]
    calls += [[close("Pc", P), close("Mc", M)], [close("Ma", M), close("Pa", P)],
              [(OWN, b * BLK, BLK, win[b][:, whole(me)], None if b == me else mate, win[b][:, whole(me)], s["w%d" % b], on_chip)
               for b in range(2)]]
    for k, call in enumerate(calls):
        for c in call:
            if c[0] not in ready:
                offsets(c[0])
        if k == 0:
            V.wait_ge(s.tab, 16 * ntab)
            S.wait_ge(s.tab, 16 * ntab)
        for Q, (place, lo, n, where, *_) in zip((V, S), call):
            Q.wait_ge(s.vec, ready[place])
            o = place * LC + lo // GRP
            copy(Q, where, T.tabs[:, 0:PART].indirect(T.off[:, o:o + n // GRP]), s["g%d" % k])
        g.wait_ge(s["g%d" % k], 2)
        send([to(c, mask, sem, where, there) for _, _, _, where, c, there, sem, mask in call if c is not None])

    def bases_of(b, q):
        slots = [nth(h, o) if x == h else (2 if x == (p, m)[b] else 3) for o, x in enumerate(owners)]
        return [(0 if k == 3 else (k + 1) * BLK) if q else k * BLK for k in slots]

    b = me
    picked = picks([(b * BC + q * QC, bases_of(b, q)) for q in range(2)], QC)
    for Q in (V, S):
        Q.wait_ge(s.vec, picked)
        Q.wait_ge(s["g%d" % (len(calls) - 1)], 2)
        Q.wait_ge(s["w%d" % b], count(on_chip) + count(off_chip))
    for q in range(2):
        c = s["c%d%d" % (b, q)]
        for i, Q in enumerate((V, S)):
            o = q * HALF + i * HALF // 2
            Q.wait_ge(s["x%d%d" % (b, q)], count(off_chip))
            copy(Q, T.res[:, b * BLK + o:b * BLK + o + HALF // 2],
                 win[b][:, view(q)].indirect(T.pick[:, o // GRP:(o + HALF // 2) // GRP]), c)
        o = b * BLK + q * HALF
        g.wait_ge(c, 2)
        send([to(mate, on_chip, s["x%d%d" % (b, q)], T.res[:, o:o + HALF], T.res[:, o:o + HALF])])
        g.sync.wait_ge(c, 2)
        g.sync.dma_start(T.y[:, o:o + HALF], T.res[:, o:o + HALF]).then_inc(s.st0, 16)
    for q in range(2):
        o = (1 - b) * BLK + q * HALF
        S.wait_ge(s["x%d%d" % (1 - b, q)], count(on_chip))
        S.dma_start(T.y[:, o:o + HALF], T.res[:, o:o + HALF]).then_inc(s.st1, 16)
    S.wait_ge(s.st1, 32)
    g.sync.wait_ge(s.st0, 32)
    g.wait_ge(s.left, nleft[0])
